import numpy as np
import ml_dtypes


def mxq(x, axis, fmt="e4m3"):
    dtype, down = {"e4m3": (ml_dtypes.float8_e4m3fn, 7), "e5m2": (ml_dtypes.float8_e5m2, 14)}[fmt]
    v = np.moveaxis(np.asarray(x, np.float32).astype(ml_dtypes.bfloat16).astype(np.float64), axis, -1)
    blocks = v.reshape(v.shape[:-1] + (-1, 32))
    amax = np.abs(blocks).max(-1, keepdims=True)
    byte = np.maximum(np.where(amax > 0, np.frexp(amax)[1] - 1 + 127, 0) - down, 1)
    scale = np.exp2(byte - 127.0)
    codes = (blocks / scale).astype(np.float32).astype(dtype).astype(np.float64)
    return np.moveaxis((codes * scale).reshape(v.shape), -1, axis)


WIDE = False


def mx_kscale(k):
    if not WIDE:
        return np.ones(k)
    levels = np.array([10, -10, 5, -5, 0])
    if k % 512:
        return np.exp2(np.random.permutation(np.resize(levels, k // 32))).repeat(32)
    a = np.empty((k // 512, 16))
    for p in range(k // 512):
        a[p, :8] = np.random.permutation(np.resize(levels, 8))
        for g in range(8):
            far = levels[np.abs(levels - a[p, g]) >= 10]
            a[p, g + 8] = far[np.random.randint(len(far))]
    return np.exp2(a.ravel()).repeat(32)


def f64(x):
    return np.asarray(x).astype(np.float64)


def striped(idx):
    return np.tile(idx.reshape(-1, 16).T, (8, 1)).astype(np.uint16)


def unstriped(offs):
    return offs[:16].T.reshape(-1).astype(np.int64)


def striped8(idx):
    return np.concatenate([x.reshape(-1, 16).T for x in idx]).astype(np.uint16)


def runs(offs, k):
    lists = np.stack([offs[16 * r : 16 * r + 16].T.reshape(-1) for r in range(8)]).astype(np.int64)
    return lists[np.arange(k) % 512 // 64]


def pack_weight(w):
    k, n = w.shape
    w = f64(np.asarray(w, np.float32).astype(ml_dtypes.bfloat16)).reshape(k // 32, 32, n)
    amax = np.abs(w).max(1)
    byte = np.clip(np.where(amax > 0, np.frexp(amax)[1] - 1 + 127 - 7, 1), 1, 254)
    scaled = (w * np.exp2(127.0 - byte)[:, None, :]).reshape(k, n).astype(np.float32)
    words = np.ascontiguousarray(scaled.reshape(k // 512, 128, 4, n).transpose(0, 1, 3, 2)).astype(ml_dtypes.float8_e4m3fn).view(np.uint8)
    return words, np.ascontiguousarray(byte.astype(np.uint8).reshape(k // 512, 16, n))


def unpack_weight(words, scales):
    g, p, n, _ = words.shape
    vals = np.ascontiguousarray(words).view(ml_dtypes.float8_e4m3fn).astype(np.float64) * np.repeat(np.exp2(scales.astype(np.float64) - 127.0), 8, axis=1)[..., None]
    return vals.transpose(0, 1, 3, 2).reshape(g * 512, n)


E2M1 = np.array([0.0, 0.5, 1.0, 1.5, 2.0, 3.0, 4.0, 6.0, -0.0, -0.5, -1.0, -1.5, -2.0, -3.0, -4.0, -6.0])


def pack_fp4(w):
    k, n = w.shape
    w = f64(np.asarray(w, np.float32).astype(ml_dtypes.bfloat16)).reshape(k // 32, 32, n)
    amax = np.abs(w).max(1)
    mant, ex = np.frexp(amax / 6.0)
    byte = np.clip(np.where(amax > 0, np.where(mant > 0.5, ex, ex - 1) + 127, 1), 1, 254)
    scaled = (w * np.exp2(127.0 - byte)[:, None, :]).reshape(k, n).astype(np.float32)
    c = np.ascontiguousarray(scaled.reshape(k // 512, 128, 4, n).transpose(0, 1, 3, 2)).astype(ml_dtypes.float4_e2m1fn).view(np.uint8) & 0xF
    words = (c[..., 0::2] | (c[..., 1::2] << 4)).reshape(k // 512, 128, 2 * n)
    return np.ascontiguousarray(words), np.ascontiguousarray(byte.astype(np.uint8).reshape(k // 512, 16, n))


def unpack_fp4(words, scales):
    g, _, n = scales.shape
    words = np.ascontiguousarray(words).reshape(g, 128, n, 2)
    nib = np.empty((g, 128, n, 4), np.uint8)
    nib[..., 0::2] = words & 0xF
    nib[..., 1::2] = words >> 4
    vals = E2M1[nib] * np.repeat(np.exp2(scales.astype(np.float64) - 127.0), 8, axis=1)[..., None]
    return vals.transpose(0, 1, 3, 2).reshape(g * 512, n)


K, T, S, N, G, H, W, U = 512, 1024, 256, 512, 2048, 512, 128, 1024


def setup_inputs():
    n = np.random.standard_normal
    s = mx_kscale(K)[:, None]
    u = mx_kscale(K)
    packed_xT = pack_weight(n((K, T)) * s)
    packed_dT = pack_weight(n((K, G)) / s)
    packed_w1 = pack_fp4(n((H, N)) / np.sqrt(H) / u[:, None])
    perm = np.random.permutation(S)
    return {
        "x_words": packed_xT[0],
        "x_scales": packed_xT[1],
        "d_words": packed_dT[0],
        "d_scales": packed_dT[1],
        "gn": (np.random.uniform(0.5, 1.5, (H, 1)) * u[:, None]).astype(np.float32),
        "w1_words": packed_w1[0],
        "w1_scales": packed_w1[1],
        "offs": striped(np.random.permutation(T)[:S]),
        "ka": striped8(np.random.randint(0, G, (8, H))),
        "kb": striped8(np.random.randint(0, G, (8, H))),
        "n1": striped(perm[:W]),
        "n2": striped(perm[W:]),
        "n3": striped(np.random.permutation(U)[:S]),
        "n4": striped(np.random.permutation(S)),
    }


def reference(x_words, x_scales, d_words, d_scales, gn, w1_words, w1_scales, offs, ka, kb, n1, n2, n3, n4):
    d_ka = unpack_weight(d_words, d_scales)[np.arange(K)[:, None], runs(ka, K)]
    xq = unpack_weight(x_words, x_scales)[:, unstriped(offs)]
    d_kb = unpack_weight(d_words, d_scales)[np.arange(K)[:, None], runs(kb, K)]
    h = 0.0625 * (d_ka.T @ xq + d_kb.T @ xq)
    pb = h[:, unstriped(n2)]
    pa = h[:, unstriped(n1)]
    rb = pb - (0.5 * pa)
    ra = np.sqrt((pa) ** 2 + (pb) ** 2 + 0.25)
    ds = np.zeros((H, S))
    ds[:, unstriped(n1)] = ra
    dt = ds.copy()
    dt[:, unstriped(n2)] = rb
    z = f64(gn) * dt
    h2 = unpack_fp4(w1_words, w1_scales).T @ mxq(z, 0, "e4m3")
    nw = np.maximum(h2, h2[:, unstriped(n4)])
    out = np.zeros((N, U))
    out[:, unstriped(n3)] = nw
    return out

@@ -1,0 +1,198 @@
+from contextlib import ExitStack
+
+import concourse.mybir as mybir
+
+F32 = mybir.dt.float32
+BF16 = mybir.dt.bfloat16
+I32 = mybir.dt.int32
+U32 = mybir.dt.uint32
+U16 = mybir.dt.uint16
+U8 = mybir.dt.uint8
+FP8X4 = mybir.dt.float8_e4m3fn_x4
+FP4X4 = mybir.dt.float4_e2m1fn_x4
+ALU = mybir.AluOpType
+COPY = mybir.ActivationFunctionType.Copy
+SQRT = mybir.ActivationFunctionType.Sqrt
+
+P = 128
+PACK = 4
+T, G, S, H, N, W, U = 1024, 2048, 256, 512, 512, 128, 1024
+ROWS = 16
+FLOPS = 2 * (2 * 512 * H * S + H * N * S)
+
+
+def tile_picked_aqlpolarpags_none_p_kernel(
+    tc, x_words, x_scales, d_words, d_scales, gn, w1_words, w1_scales, offs, ka, kb, n1, n2, n3, n4, out
+):
+    nc = tc.nc
+    with ExitStack() as ctx:
+        keep = ctx.enter_context(tc.tile_pool(name="keep", bufs=1))
+        psum = ctx.enter_context(tc.psum_pool(name="psum", bufs=1))
+
+        def load_list(name, src):
+            tile = keep.tile(list(src.shape), U16, name=name)
+            nc.sync.dma_start(tile[:], src)
+            return tile
+
+        def load_scale_rows(name, src, width):
+            tile = keep.tile([P, width], U8, name=name, align_bytes=64)
+            rows = src[0].bitcast(I32).unsqueeze(1).broadcast_to([ROWS, P // ROWS, width // 4])
+            nc.sync.dma_start(tile[:].bitcast(I32), rows)
+            return tile
+
+        def load_words(name, src, width):
+            tile = keep.tile([P, width], U32, name=name, align_bytes=64)
+            nc.sync.dma_start(tile[:].bitcast(I32), src[0].rearrange("p n t -> p (n t)").bitcast(I32))
+            return tile
+
+        ka_list = load_list("ka_list", ka)
+        d_byte_table = load_scale_rows("d_byte_table", d_scales, G)
+        kb_list = load_list("kb_list", kb)
+        offs_list = load_list("offs_list", offs)
+        x_byte_table = load_scale_rows("x_byte_table", x_scales, T)
+        d_word_table = load_words("d_word_table", d_words, G)
+        x_word_table = load_words("x_word_table", x_words, T)
+        n1_list = load_list("n1_list", n1)
+        n2_list = load_list("n2_list", n2)
+        gain = keep.tile([P, PACK], F32, name="gain")
+        nc.sync.dma_start(gain[:], gn.rearrange("(p t) o -> p (t o)", t=PACK))
+        w1_codes = keep.tile([P, 2 * N], U8, name="w1_codes", align_bytes=64)
+        nc.sync.dma_start(w1_codes[:].bitcast(I32), w1_words[0].bitcast(I32))
+        w1_plane = keep.tile([P, N], U8, name="w1_plane", align_bytes=64)
+        nc.vector.memset(w1_plane[:].bitcast(I32), 0)
+        for q in range(4):
+            nc.sync.dma_start(
+                w1_plane[32 * q : 32 * q + 4, :].bitcast(I32), w1_scales[0, 4 * q : 4 * q + 4, :].bitcast(I32)
+            )
+        n4_list = load_list("n4_list", n4)
+        n3_list = load_list("n3_list", n3)
+
+        d_bytes = keep.tile([P, 2, H], U8, name="d_bytes", align_bytes=64)
+        x_bytes = keep.tile([P, S], U8, name="x_bytes", align_bytes=64)
+        for a, codes in enumerate((ka_list, kb_list)):
+            nc.vector.tensor_copy(d_bytes[:, a, :], d_byte_table[:].indirect(codes[:]))
+        nc.vector.tensor_copy(x_bytes[:], x_byte_table[:].indirect(offs_list[:]))
+        plane = keep.tile([P, 2 * H + S], U8, name="plane", align_bytes=64)
+        nc.vector.tensor_copy(
+            plane[:, : 2 * H].rearrange("p (a t m) -> p a t m", a=2, t=PACK),
+            d_bytes[:].rearrange("p a (m t) -> p a t m", t=PACK),
+        )
+        nc.vector.tensor_copy(plane[:, 2 * H :].bitcast(I32), x_bytes[:].bitcast(I32))
+        for i, queue in ((1, nc.sync), (2, nc.scalar), (3, nc.sync)):
+            queue.dma_start(plane[i:P:32, :].bitcast(I32), plane[8 * i : P : 32, :].bitcast(I32))
+
+        d_picked = keep.tile([P, 2, H], U32, name="d_picked", align_bytes=64)
+        d_dealt = keep.tile([P, 2, H], U32, name="d_dealt", align_bytes=64)
+        x_picked = keep.tile([P, S], U32, name="x_picked", align_bytes=64)
+
+        def deal_words(a):
+            nc.vector.tensor_copy(
+                d_dealt[:, a, :].bitcast(I32).rearrange("p (t c i) -> p c t i", t=PACK, i=4),
+                d_picked[:, a, :].bitcast(I32).rearrange("p (c i t) -> p c t i", t=PACK, i=4),
+            )
+
+        nc.vector.tensor_copy(d_picked[:, 0, :], d_word_table[:].indirect(ka_list[:]))
+        nc.vector.tensor_copy(d_picked[:, 1, :], d_word_table[:].indirect(kb_list[:]))
+        deal_words(0)
+        nc.vector.tensor_copy(x_picked[:], x_word_table[:].indirect(offs_list[:]))
+        deal_words(1)
+
+        h_bank = [psum.tile([P, S], F32, name=f"h_bank{t}") for t in range(PACK)]
+        for t in range(PACK):
+            for a in range(2):
+                nc.tensor.matmul_mx(
+                    out=h_bank[t][:],
+                    lhsT=d_dealt[:, a, t * P : (t + 1) * P].bitcast(FP8X4),
+                    lhsT_scale=plane[:, a * H + t * P : a * H + (t + 1) * P],
+                    rhs=x_picked[:].bitcast(FP8X4),
+                    rhs_scale=plane[:, 2 * H :],
+                    start=(a == 0),
+                    stop=(a == 1),
+                )
+
+        h = [keep.tile([P, S], F32, name=f"h{t}") for t in range(PACK)]
+        pair = [keep.tile([P, 2 * W], F32, name=f"pair{t}") for t in range(PACK)]
+        squares = [keep.tile([P, 2 * W], F32, name=f"squares{t}") for t in range(PACK)]
+        radicand = [keep.tile([P, W], F32, name=f"radicand{t}") for t in range(PACK)]
+        ra = [keep.tile([P, W], F32, name=f"ra{t}") for t in range(PACK)]
+        rb = [keep.tile([P, W], F32, name=f"rb{t}") for t in range(PACK)]
+        dt = [keep.tile([P, S], F32, name=f"dt{t}") for t in range(PACK)]
+        z = keep.tile([P, S, PACK], BF16, name="z", align_bytes=64)
+
+        def fetch_pairs(t):
+            if t == 0:
+                nc.scalar.activation(h[t][:], h_bank[t][:], COPY, scale=0.0625)
+            else:
+                nc.vector.tensor_scalar(h[t][:], h_bank[t][:], 0.0625, None, ALU.mult)
+            nc.scalar.activation(pair[t][:, :W], h[t][:].indirect(n1_list[:]), COPY)
+            nc.scalar.activation(pair[t][:, W:], h[t][:].indirect(n2_list[:]), COPY)
+
+        def polar(t):
+            pa, pb = pair[t][:, :W], pair[t][:, W:]
+            nc.vector.scalar_tensor_tensor(rb[t][:], pa, -0.5, pb, ALU.mult, ALU.add)
+            nc.vector.tensor_tensor(squares[t][:], pair[t][:], pair[t][:], ALU.mult)
+            nc.vector.scalar_tensor_tensor(
+                radicand[t][:], squares[t][:, :W], 0.25, squares[t][:, W:], ALU.add, ALU.add
+            )
+
+        def put_rb(t):
+            nc.scalar.activation(ra[t][:], radicand[t][:], SQRT)
+            nc.scalar.activation(dt[t][:].indirect(n2_list[:]), rb[t][:], COPY)
+
+        def put_ra(t):
+            nc.scalar.activation(dt[t][:].indirect(n1_list[:]), ra[t][:], COPY)
+            nc.vector.tensor_scalar(z[:, :, t], dt[t][:], gain[:, t : t + 1], None, ALU.mult)
+
+        for step in range(PACK + 2):
+            if step < PACK:
+                fetch_pairs(step)
+                polar(step)
+            if 1 <= step <= PACK:
+                put_rb(step - 1)
+            if step >= 2:
+                put_ra(step - 2)
+
+        z_codes = keep.tile([P, S], U32, name="z_codes", align_bytes=64)
+        z_plane = keep.tile([P, S], U8, name="z_plane", align_bytes=64)
+        nc.vector.quantize_mx(
+            out=z_codes[:].bitcast(FP8X4), scales=z_plane[:], in_=z[:].rearrange("p s t -> p (s t)")
+        )
+
+        blocks = N // P
+        h2_bank = [psum.tile([P, S], F32, name=f"h2_bank{u}") for u in range(blocks)]
+        h2 = [keep.tile([P, S], F32, name=f"h2_{u}") for u in range(blocks)]
+        other = [keep.tile([P, S], F32, name=f"other{u}") for u in range(blocks)]
+        nw = [keep.tile([P, S], F32, name=f"nw{u}") for u in range(blocks)]
+        page = [keep.tile([P, U], F32, name=f"page{u}") for u in range(blocks)]
+        for u in range(blocks):
+            nc.tensor.matmul_mx(
+                out=h2_bank[u][:],
+                lhsT=w1_codes[:, 2 * u * P : 2 * (u + 1) * P].bitcast(FP4X4),
+                lhsT_scale=w1_plane[:, u * P : (u + 1) * P],
+                rhs=z_codes[:].bitcast(FP8X4),
+                rhs_scale=z_plane[:],
+                start=True,
+                stop=True,
+            )
+
+        def fetch_other(u):
+            if u == 0:
+                nc.scalar.activation(h2[u][:], h2_bank[u][:], COPY)
+            else:
+                nc.vector.tensor_copy(h2[u][:], h2_bank[u][:])
+            for c in range(2):
+                nc.scalar.activation(
+                    other[u][:, c * W : (c + 1) * W], h2[u][:].indirect(n4_list[:, c * 8 : (c + 1) * 8]), COPY
+                )
+            nc.vector.tensor_tensor(nw[u][:], h2[u][:], other[u][:], ALU.max)
+
+        def put_page(u):
+            nc.vector.memset(page[u][:], 0.0)
+            nc.scalar.activation(page[u][:].indirect(n3_list[:]), nw[u][:], COPY)
+            nc.sync.dma_start(out[u * P : (u + 1) * P, :], page[u][:])
+
+        for step in range(blocks + 1):
+            if step < blocks:
+                fetch_other(step)
+            if step >= 1:
+                put_page(step - 1)

@@ -18,6 +18,7 @@ P = 128
 PACK = 4
 T, G, S, H, N, W, U = 1024, 2048, 256, 512, 512, 128, 1024
 ROWS = 16
+SPARE = 16
 FLOPS = 2 * (2 * 512 * H * S + H * N * S)
 
 
@@ -35,7 +36,7 @@ def tile_picked_aqlpolarpags_none_p_kernel(
             return tile
 
         def load_scale_rows(name, src, width):
-            tile = keep.tile([P, width], U8, name=name, align_bytes=64)
+            tile = keep.tile([P, width], U8, name=name, tag=name, align_bytes=64)
             rows = src[0].bitcast(I32).unsqueeze(1).broadcast_to([ROWS, P // ROWS, width // 4])
             nc.sync.dma_start(tile[:].bitcast(I32), rows)
             return tile
@@ -45,67 +46,70 @@ def tile_picked_aqlpolarpags_none_p_kernel(
             nc.sync.dma_start(tile[:].bitcast(I32), src[0].rearrange("p n t -> p (n t)").bitcast(I32))
             return tile
 
+        warm_in = keep.tile([P, 1], F32, name="warm_in")
+        warm_out = keep.tile([P, 1], F32, name="warm_out")
+        nc.vector.memset(warm_in[:], 1.0)
+        nc.scalar.activation(warm_out[:], warm_in[:], SQRT)
+
+        offs_list = load_list("offs_list", offs)
+        x_byte_table = load_scale_rows("x_byte_table", x_scales, T)
         ka_list = load_list("ka_list", ka)
         d_byte_table = load_scale_rows("d_byte_table", d_scales, G)
         kb_list = load_list("kb_list", kb)
-        offs_list = load_list("offs_list", offs)
-        x_byte_table = load_scale_rows("x_byte_table", x_scales, T)
+        n1_list = load_list("n1_list", n1)
         d_word_table = load_words("d_word_table", d_words, G)
         x_word_table = load_words("x_word_table", x_words, T)
-        n1_list = load_list("n1_list", n1)
         n2_list = load_list("n2_list", n2)
+        n4_list = load_list("n4_list", n4)
+        n3_list = load_list("n3_list", n3)
         gain = keep.tile([P, PACK], F32, name="gain")
-        nc.sync.dma_start(gain[:], gn.rearrange("(p t) o -> p (t o)", t=PACK))
-        w1_codes = keep.tile([P, 2 * N], U8, name="w1_codes", align_bytes=64)
-        nc.sync.dma_start(w1_codes[:].bitcast(I32), w1_words[0].bitcast(I32))
-        w1_plane = keep.tile([P, N], U8, name="w1_plane", align_bytes=64)
-        nc.vector.memset(w1_plane[:].bitcast(I32), 0)
+        nc.gpsimd.dma_start(gain[:], gn.rearrange("(p t) o -> p (t o)", t=PACK))
+
+        picked_bytes = keep.tile([P, 2 * H + S], U8, name="picked_bytes", tag="picked_bytes", align_bytes=64)
+        moved_bytes = keep.tile([P, 2 * H + S], U8, name="moved_bytes", align_bytes=64)
+        nc.vector.memset(moved_bytes[:].bitcast(I32), 0)
+        nc.vector.tensor_copy(picked_bytes[:, 2 * H :], x_byte_table[:].indirect(offs_list[:]))
+        for a, codes in enumerate((ka_list, kb_list)):
+            nc.vector.tensor_copy(picked_bytes[:, a * H : (a + 1) * H], d_byte_table[:].indirect(codes[:]))
+        for q, queue in enumerate((nc.sync, nc.scalar, nc.sync, nc.scalar)):
+            queue.dma_start(
+                moved_bytes[32 * q : 32 * q + 4, :].bitcast(I32),
+                picked_bytes[32 * q : 32 * q + 32 : 8, :].bitcast(I32),
+            )
+
+        w1_plane = keep.tile([P, N], U8, name="w1_plane", tag="d_byte_table", align_bytes=64)
+        nc.gpsimd.memset(w1_plane[:].bitcast(I32), 0)
         for q in range(4):
             nc.sync.dma_start(
                 w1_plane[32 * q : 32 * q + 4, :].bitcast(I32), w1_scales[0, 4 * q : 4 * q + 4, :].bitcast(I32)
             )
-        n4_list = load_list("n4_list", n4)
-        n3_list = load_list("n3_list", n3)
-
-        d_bytes = keep.tile([P, 2, H], U8, name="d_bytes", align_bytes=64)
-        x_bytes = keep.tile([P, S], U8, name="x_bytes", align_bytes=64)
-        for a, codes in enumerate((ka_list, kb_list)):
-            nc.vector.tensor_copy(d_bytes[:, a, :], d_byte_table[:].indirect(codes[:]))
-        nc.vector.tensor_copy(x_bytes[:], x_byte_table[:].indirect(offs_list[:]))
-        plane = keep.tile([P, 2 * H + S], U8, name="plane", align_bytes=64)
-        nc.vector.tensor_copy(
-            plane[:, : 2 * H].rearrange("p (a t m) -> p a t m", a=2, t=PACK),
-            d_bytes[:].rearrange("p a (m t) -> p a t m", t=PACK),
-        )
-        nc.vector.tensor_copy(plane[:, 2 * H :].bitcast(I32), x_bytes[:].bitcast(I32))
-        for i, queue in ((1, nc.sync), (2, nc.scalar), (3, nc.sync)):
-            queue.dma_start(plane[i:P:32, :].bitcast(I32), plane[8 * i : P : 32, :].bitcast(I32))
+        w1_codes = keep.tile([P, 2 * N], U8, name="w1_codes", tag="picked_bytes", align_bytes=64)
+        nc.sync.dma_start(w1_codes[:].bitcast(I32), w1_words[0].bitcast(I32))
 
         d_picked = keep.tile([P, 2, H], U32, name="d_picked", align_bytes=64)
-        d_dealt = keep.tile([P, 2, H], U32, name="d_dealt", align_bytes=64)
         x_picked = keep.tile([P, S], U32, name="x_picked", align_bytes=64)
-
-        def deal_words(a):
-            nc.vector.tensor_copy(
-                d_dealt[:, a, :].bitcast(I32).rearrange("p (t c i) -> p c t i", t=PACK, i=4),
-                d_picked[:, a, :].bitcast(I32).rearrange("p (c i t) -> p c t i", t=PACK, i=4),
-            )
-
         nc.vector.tensor_copy(d_picked[:, 0, :], d_word_table[:].indirect(ka_list[:]))
         nc.vector.tensor_copy(d_picked[:, 1, :], d_word_table[:].indirect(kb_list[:]))
-        deal_words(0)
         nc.vector.tensor_copy(x_picked[:], x_word_table[:].indirect(offs_list[:]))
-        deal_words(1)
 
-        h_bank = [psum.tile([P, S], F32, name=f"h_bank{t}") for t in range(PACK)]
-        for t in range(PACK):
+        h_bank = [psum.tile([P, S], F32, name=f"h_bank{t}", tag=f"h_bank{t}") for t in range(PACK)]
+
+        def first_product(t):
+            words = keep.tile([P, 2, P], U32, name=f"dealt_words{t}", align_bytes=64)
+            plane = keep.tile([P, 2, P], U8, name=f"dealt_bytes{t}", align_bytes=64)
+            nc.vector.tensor_copy(
+                words[:].bitcast(I32), d_picked[:].bitcast(I32).rearrange("p a (m t) -> p a m t", t=PACK)[:, :, :, t]
+            )
+            nc.vector.tensor_copy(
+                plane[:], moved_bytes[:, : 2 * H].rearrange("p (a m t) -> p a m t", a=2, t=PACK)[:, :, :, t]
+            )
             for a in range(2):
                 nc.tensor.matmul_mx(
                     out=h_bank[t][:],
-                    lhsT=d_dealt[:, a, t * P : (t + 1) * P].bitcast(FP8X4),
-                    lhsT_scale=plane[:, a * H + t * P : a * H + (t + 1) * P],
+                    lhsT=words[:, a, :].bitcast(FP8X4),
+                    lhsT_scale=plane[:, a, :],
                     rhs=x_picked[:].bitcast(FP8X4),
-                    rhs_scale=plane[:, 2 * H :],
+                    rhs_scale=moved_bytes[:, 2 * H :],
                     start=(a == 0),
                     stop=(a == 1),
                 )
@@ -119,7 +123,11 @@ def tile_picked_aqlpolarpags_none_p_kernel(
         dt = [keep.tile([P, S], F32, name=f"dt{t}") for t in range(PACK)]
         z = keep.tile([P, S, PACK], BF16, name="z", align_bytes=64)
 
+        halves = [slice(0, S // 2), slice(S // 2, S)]
+
         def fetch_pairs(t):
+            if t + 1 < PACK:
+                first_product(t + 1)
             if t == 0:
                 nc.scalar.activation(h[t][:], h_bank[t][:], COPY, scale=0.0625)
             else:
@@ -136,13 +144,15 @@ def tile_picked_aqlpolarpags_none_p_kernel(
             )
 
         def put_rb(t):
-            nc.scalar.activation(ra[t][:], radicand[t][:], SQRT)
             nc.scalar.activation(dt[t][:].indirect(n2_list[:]), rb[t][:], COPY)
+            nc.scalar.activation(ra[t][:], radicand[t][:], SQRT)
 
         def put_ra(t):
             nc.scalar.activation(dt[t][:].indirect(n1_list[:]), ra[t][:], COPY)
-            nc.vector.tensor_scalar(z[:, :, t], dt[t][:], gain[:, t : t + 1], None, ALU.mult)
+            for cols in halves if t == PACK - 1 else [slice(0, S)]:
+                nc.vector.tensor_scalar(z[:, cols, t], dt[t][:, cols], gain[:, t : t + 1], None, ALU.mult)
 
+        first_product(0)
         for step in range(PACK + 2):
             if step < PACK:
                 fetch_pairs(step)
@@ -154,40 +164,45 @@ def tile_picked_aqlpolarpags_none_p_kernel(
 
         z_codes = keep.tile([P, S], U32, name="z_codes", align_bytes=64)
         z_plane = keep.tile([P, S], U8, name="z_plane", align_bytes=64)
-        nc.vector.quantize_mx(
-            out=z_codes[:].bitcast(FP8X4), scales=z_plane[:], in_=z[:].rearrange("p s t -> p (s t)")
-        )
+        for cols in halves:
+            nc.vector.quantize_mx(
+                out=z_codes[:, cols].bitcast(FP8X4),
+                scales=z_plane[:, cols],
+                in_=z[:, cols, :].rearrange("p s t -> p (s t)"),
+            )
 
         blocks = N // P
-        h2_bank = [psum.tile([P, S], F32, name=f"h2_bank{u}") for u in range(blocks)]
-        h2 = [keep.tile([P, S], F32, name=f"h2_{u}") for u in range(blocks)]
+        h2 = [keep.tile([P, S + SPARE], F32, name=f"h2_{u}") for u in range(blocks)]
         other = [keep.tile([P, S], F32, name=f"other{u}") for u in range(blocks)]
         nw = [keep.tile([P, S], F32, name=f"nw{u}") for u in range(blocks)]
         page = [keep.tile([P, U], F32, name=f"page{u}") for u in range(blocks)]
-        for u in range(blocks):
+        nc.gpsimd.memset(page[0][:], 0.0)
+        for u in range(1, blocks):
+            nc.scalar.copy(page[u][:], page[0][:])
+
+        def second_product(u, cols, tag):
+            bank = psum.tile([P, cols.stop - cols.start], F32, name="h2_bank", tag=tag)
             nc.tensor.matmul_mx(
-                out=h2_bank[u][:],
+                out=bank[:],
                 lhsT=w1_codes[:, 2 * u * P : 2 * (u + 1) * P].bitcast(FP4X4),
                 lhsT_scale=w1_plane[:, u * P : (u + 1) * P],
-                rhs=z_codes[:].bitcast(FP8X4),
-                rhs_scale=z_plane[:],
+                rhs=z_codes[:, cols].bitcast(FP8X4),
+                rhs_scale=z_plane[:, cols],
                 start=True,
                 stop=True,
             )
+            return bank
 
         def fetch_other(u):
             if u == 0:
-                nc.scalar.activation(h2[u][:], h2_bank[u][:], COPY)
+                for c, cols in enumerate(halves):
+                    nc.scalar.activation(h2[u][:, cols], second_product(u, cols, f"half_bank{c}")[:], COPY)
             else:
-                nc.vector.tensor_copy(h2[u][:], h2_bank[u][:])
-            for c in range(2):
-                nc.scalar.activation(
-                    other[u][:, c * W : (c + 1) * W], h2[u][:].indirect(n4_list[:, c * 8 : (c + 1) * 8]), COPY
-                )
-            nc.vector.tensor_tensor(nw[u][:], h2[u][:], other[u][:], ALU.max)
+                nc.vector.tensor_copy(h2[u][:, :S], second_product(u, slice(0, S), f"h_bank{u}")[:])
+            nc.scalar.activation(other[u][:], h2[u][:].indirect(n4_list[:]), COPY)
+            nc.vector.tensor_tensor(nw[u][:], h2[u][:, :S], other[u][:], ALU.max)
 
         def put_page(u):
-            nc.vector.memset(page[u][:], 0.0)
             nc.scalar.activation(page[u][:].indirect(n3_list[:]), nw[u][:], COPY)
             nc.sync.dma_start(out[u * P : (u + 1) * P, :], page[u][:])
 

@@ -35,10 +35,10 @@ def tile_picked_aqlpolarpags_none_p_kernel(
             nc.sync.dma_start(tile[:], src)
             return tile
 
-        def load_scale_rows(name, src, width):
+        def load_scale_rows(name, src, width, clearer):
             tile = keep.tile([P, width], U8, name=name, tag=name, align_bytes=64)
-            rows = src[0].bitcast(I32).unsqueeze(1).broadcast_to([ROWS, P // ROWS, width // 4])
-            nc.sync.dma_start(tile[:].bitcast(I32), rows)
+            clearer.memset(tile[:].bitcast(I32), 0)
+            nc.sync.dma_start(tile[0 : P : P // ROWS, :].bitcast(I32), src[0].bitcast(I32))
             return tile
 
         def load_words(name, src, width):
@@ -46,17 +46,12 @@ def tile_picked_aqlpolarpags_none_p_kernel(
             nc.sync.dma_start(tile[:].bitcast(I32), src[0].rearrange("p n t -> p (n t)").bitcast(I32))
             return tile
 
-        warm_in = keep.tile([P, 1], F32, name="warm_in")
-        warm_out = keep.tile([P, 1], F32, name="warm_out")
-        nc.vector.memset(warm_in[:], 1.0)
-        nc.scalar.activation(warm_out[:], warm_in[:], SQRT)
-
         offs_list = load_list("offs_list", offs)
-        x_byte_table = load_scale_rows("x_byte_table", x_scales, T)
         ka_list = load_list("ka_list", ka)
-        d_byte_table = load_scale_rows("d_byte_table", d_scales, G)
         kb_list = load_list("kb_list", kb)
         n1_list = load_list("n1_list", n1)
+        x_byte_table = load_scale_rows("x_byte_table", x_scales, T, nc.gpsimd)
+        d_byte_table = load_scale_rows("d_byte_table", d_scales, G, nc.vector)
         d_word_table = load_words("d_word_table", d_words, G)
         x_word_table = load_words("x_word_table", x_words, T)
         n2_list = load_list("n2_list", n2)
@@ -64,6 +59,11 @@ def tile_picked_aqlpolarpags_none_p_kernel(
         n3_list = load_list("n3_list", n3)
         gain = keep.tile([P, PACK], F32, name="gain")
         nc.gpsimd.dma_start(gain[:], gn.rearrange("(p t) o -> p (t o)", t=PACK))
+
+        warm_in = keep.tile([P, 1], F32, name="warm_in")
+        warm_out = keep.tile([P, 1], F32, name="warm_out")
+        nc.vector.memset(warm_in[:], 1.0)
+        nc.scalar.activation(warm_out[:], warm_in[:], SQRT)
 
         picked_bytes = keep.tile([P, 2 * H + S], U8, name="picked_bytes", tag="picked_bytes", align_bytes=64)
         moved_bytes = keep.tile([P, 2 * H + S], U8, name="moved_bytes", align_bytes=64)

@@ -42,7 +42,7 @@ def tile_picked_aqlpolarpags_none_p_kernel(
             return tile
 
         def load_words(name, src, width):
-            tile = keep.tile([P, width], U32, name=name, align_bytes=64)
+            tile = keep.tile([P, width], U32, name=name, tag=name, align_bytes=64)
             nc.sync.dma_start(tile[:].bitcast(I32), src[0].rearrange("p n t -> p (n t)").bitcast(I32))
             return tile
 
@@ -77,16 +77,10 @@ def tile_picked_aqlpolarpags_none_p_kernel(
                 picked_bytes[32 * q : 32 * q + 32 : 8, :].bitcast(I32),
             )
 
-        w1_plane = keep.tile([P, N], U8, name="w1_plane", tag="d_byte_table", align_bytes=64)
-        nc.gpsimd.memset(w1_plane[:].bitcast(I32), 0)
-        for q in range(4):
-            nc.sync.dma_start(
-                w1_plane[32 * q : 32 * q + 4, :].bitcast(I32), w1_scales[0, 4 * q : 4 * q + 4, :].bitcast(I32)
-            )
-        w1_codes = keep.tile([P, 2 * N], U8, name="w1_codes", tag="picked_bytes", align_bytes=64)
+        w1_codes = keep.tile([P, 2 * N], U8, name="w1_codes", tag="d_word_table", align_bytes=64)
         nc.sync.dma_start(w1_codes[:].bitcast(I32), w1_words[0].bitcast(I32))
 
-        d_picked = keep.tile([P, 2, H], U32, name="d_picked", align_bytes=64)
+        d_picked = keep.tile([P, 2, H], U32, name="d_picked", tag="d_picked", align_bytes=64)
         x_picked = keep.tile([P, S], U32, name="x_picked", align_bytes=64)
         nc.vector.tensor_copy(d_picked[:, 0, :], d_word_table[:].indirect(ka_list[:]))
         nc.vector.tensor_copy(d_picked[:, 1, :], d_word_table[:].indirect(kb_list[:]))
@@ -94,11 +88,14 @@ def tile_picked_aqlpolarpags_none_p_kernel(
 
         h_bank = [psum.tile([P, S], F32, name=f"h_bank{t}", tag=f"h_bank{t}") for t in range(PACK)]
 
+        first_words = keep.tile([P, 2, P], U32, name="first_words", align_bytes=64)
+        later_words = keep.tile([P, PACK - 1, 2, P], U32, name="later_words", tag="picked_bytes", align_bytes=64)
+
         def first_product(t):
-            words = keep.tile([P, 2, P], U32, name=f"dealt_words{t}", align_bytes=64)
+            words = first_words[:] if t == 0 else later_words[:, t - 1]
             plane = keep.tile([P, 2, P], U8, name=f"dealt_bytes{t}", align_bytes=64)
             nc.vector.tensor_copy(
-                words[:].bitcast(I32), d_picked[:].bitcast(I32).rearrange("p a (m t) -> p a m t", t=PACK)[:, :, :, t]
+                words.bitcast(I32), d_picked[:].bitcast(I32).rearrange("p a (m t) -> p a m t", t=PACK)[:, :, :, t]
             )
             nc.vector.tensor_copy(
                 plane[:], moved_bytes[:, : 2 * H].rearrange("p (a m t) -> p a m t", a=2, t=PACK)[:, :, :, t]
@@ -162,6 +159,13 @@ def tile_picked_aqlpolarpags_none_p_kernel(
             if step >= 2:
                 put_ra(step - 2)
 
+        w1_plane = keep.tile([P, N], U8, name="w1_plane", tag="d_picked", align_bytes=64)
+        nc.gpsimd.memset(w1_plane[:].bitcast(I32), 0)
+        for q in range(4):
+            nc.sync.dma_start(
+                w1_plane[32 * q : 32 * q + 4, :].bitcast(I32), w1_scales[0, 4 * q : 4 * q + 4, :].bitcast(I32)
+            )
+
         z_codes = keep.tile([P, S], U32, name="z_codes", align_bytes=64)
         z_plane = keep.tile([P, S], U8, name="z_plane", align_bytes=64)
         for cols in halves:
@@ -176,7 +180,7 @@ def tile_picked_aqlpolarpags_none_p_kernel(
         other = [keep.tile([P, S], F32, name=f"other{u}") for u in range(blocks)]
         nw = [keep.tile([P, S], F32, name=f"nw{u}") for u in range(blocks)]
         page = [keep.tile([P, U], F32, name=f"page{u}") for u in range(blocks)]
-        nc.gpsimd.memset(page[0][:], 0.0)
+        nc.vector.memset(page[0][:], 0.0)
         for u in range(1, blocks):
             nc.scalar.copy(page[u][:], page[0][:])
 
@@ -206,8 +210,8 @@ def tile_picked_aqlpolarpags_none_p_kernel(
             nc.scalar.activation(page[u][:].indirect(n3_list[:]), nw[u][:], COPY)
             nc.sync.dma_start(out[u * P : (u + 1) * P, :], page[u][:])
 
-        for step in range(blocks + 1):
+        for step in range(blocks + 2):
             if step < blocks:
                 fetch_other(step)
-            if step >= 1:
-                put_page(step - 1)
+            if step >= 2:
+                put_page(step - 2)

from contextlib import ExitStack

import concourse.mybir as mybir

F32 = mybir.dt.float32
BF16 = mybir.dt.bfloat16
I32 = mybir.dt.int32
U32 = mybir.dt.uint32
U16 = mybir.dt.uint16
U8 = mybir.dt.uint8
FP8X4 = mybir.dt.float8_e4m3fn_x4
FP4X4 = mybir.dt.float4_e2m1fn_x4
ALU = mybir.AluOpType
COPY = mybir.ActivationFunctionType.Copy
SQRT = mybir.ActivationFunctionType.Sqrt

P = 128
PACK = 4
T, G, S, H, N, W, U = 1024, 2048, 256, 512, 512, 128, 1024
ROWS = 16
SPARE = 16
FLOPS = 2 * (2 * 512 * H * S + H * N * S)


def tile_picked_aqlpolarpags_none_p_kernel(
    tc, x_words, x_scales, d_words, d_scales, gn, w1_words, w1_scales, offs, ka, kb, n1, n2, n3, n4, out
):
    nc = tc.nc
    with ExitStack() as ctx:
        keep = ctx.enter_context(tc.tile_pool(name="keep", bufs=1))
        psum = ctx.enter_context(tc.psum_pool(name="psum", bufs=1))

        def load_list(name, src):
            tile = keep.tile(list(src.shape), U16, name=name)
            nc.sync.dma_start(tile[:], src)
            return tile

        def load_scale_rows(name, src, width, clearer):
            tile = keep.tile([P, width], U8, name=name, tag=name, align_bytes=64)
            clearer.memset(tile[:].bitcast(I32), 0)
            nc.sync.dma_start(tile[0 : P : P // ROWS, :].bitcast(I32), src[0].bitcast(I32))
            return tile

        def load_words(name, src, width):
            tile = keep.tile([P, width], U32, name=name, tag=name, align_bytes=64)
            nc.sync.dma_start(tile[:].bitcast(I32), src[0].rearrange("p n t -> p (n t)").bitcast(I32))
            return tile

        offs_list = load_list("offs_list", offs)
        ka_list = load_list("ka_list", ka)
        kb_list = load_list("kb_list", kb)
        n1_list = load_list("n1_list", n1)
        x_byte_table = load_scale_rows("x_byte_table", x_scales, T, nc.gpsimd)
        d_byte_table = load_scale_rows("d_byte_table", d_scales, G, nc.vector)
        d_word_table = load_words("d_word_table", d_words, G)
        x_word_table = load_words("x_word_table", x_words, T)
        n2_list = load_list("n2_list", n2)
        n4_list = load_list("n4_list", n4)
        n3_list = load_list("n3_list", n3)
        gain = keep.tile([P, PACK], F32, name="gain")
        nc.gpsimd.dma_start(gain[:], gn.rearrange("(p t) o -> p (t o)", t=PACK))

        warm_in = keep.tile([P, 1], F32, name="warm_in")
        warm_out = keep.tile([P, 1], F32, name="warm_out")
        nc.vector.memset(warm_in[:], 1.0)
        nc.scalar.activation(warm_out[:], warm_in[:], SQRT)

        picked_bytes = keep.tile([P, 2 * H + S], U8, name="picked_bytes", tag="picked_bytes", align_bytes=64)
        moved_bytes = keep.tile([P, 2 * H + S], U8, name="moved_bytes", align_bytes=64)
        nc.vector.memset(moved_bytes[:].bitcast(I32), 0)
        nc.vector.tensor_copy(picked_bytes[:, 2 * H :], x_byte_table[:].indirect(offs_list[:]))
        for a, codes in enumerate((ka_list, kb_list)):
            nc.vector.tensor_copy(picked_bytes[:, a * H : (a + 1) * H], d_byte_table[:].indirect(codes[:]))
        for q, queue in enumerate((nc.sync, nc.scalar, nc.sync, nc.scalar)):
            queue.dma_start(
                moved_bytes[32 * q : 32 * q + 4, :].bitcast(I32),
                picked_bytes[32 * q : 32 * q + 32 : 8, :].bitcast(I32),
            )

        w1_codes = keep.tile([P, 2 * N], U8, name="w1_codes", tag="d_word_table", align_bytes=64)
        nc.sync.dma_start(w1_codes[:].bitcast(I32), w1_words[0].bitcast(I32))

        d_picked = keep.tile([P, 2, H], U32, name="d_picked", tag="d_picked", align_bytes=64)
        x_picked = keep.tile([P, S], U32, name="x_picked", align_bytes=64)
        nc.vector.tensor_copy(d_picked[:, 0, :], d_word_table[:].indirect(ka_list[:]))
        nc.vector.tensor_copy(d_picked[:, 1, :], d_word_table[:].indirect(kb_list[:]))
        nc.vector.tensor_copy(x_picked[:], x_word_table[:].indirect(offs_list[:]))

        h_bank = [psum.tile([P, S], F32, name=f"h_bank{t}", tag=f"h_bank{t}") for t in range(PACK)]

        first_words = keep.tile([P, 2, P], U32, name="first_words", align_bytes=64)
        later_words = keep.tile([P, PACK - 1, 2, P], U32, name="later_words", tag="picked_bytes", align_bytes=64)

        def first_product(t):
            words = first_words[:] if t == 0 else later_words[:, t - 1]
            plane = keep.tile([P, 2, P], U8, name=f"dealt_bytes{t}", align_bytes=64)
            nc.vector.tensor_copy(
                words.bitcast(I32), d_picked[:].bitcast(I32).rearrange("p a (m t) -> p a m t", t=PACK)[:, :, :, t]
            )
            nc.vector.tensor_copy(
                plane[:], moved_bytes[:, : 2 * H].rearrange("p (a m t) -> p a m t", a=2, t=PACK)[:, :, :, t]
            )
            for a in range(2):
                nc.tensor.matmul_mx(
                    out=h_bank[t][:],
                    lhsT=words[:, a, :].bitcast(FP8X4),
                    lhsT_scale=plane[:, a, :],
                    rhs=x_picked[:].bitcast(FP8X4),
                    rhs_scale=moved_bytes[:, 2 * H :],
                    start=(a == 0),
                    stop=(a == 1),
                )

        h = [keep.tile([P, S], F32, name=f"h{t}") for t in range(PACK)]
        pair = [keep.tile([P, 2 * W], F32, name=f"pair{t}") for t in range(PACK)]
        squares = [keep.tile([P, 2 * W], F32, name=f"squares{t}") for t in range(PACK)]
        radicand = [keep.tile([P, W], F32, name=f"radicand{t}") for t in range(PACK)]
        ra = [keep.tile([P, W], F32, name=f"ra{t}") for t in range(PACK)]
        rb = [keep.tile([P, W], F32, name=f"rb{t}") for t in range(PACK)]
        dt = [keep.tile([P, S], F32, name=f"dt{t}") for t in range(PACK)]
        z = keep.tile([P, S, PACK], BF16, name="z", align_bytes=64)

        halves = [slice(0, S // 2), slice(S // 2, S)]

        def fetch_pairs(t):
            if t + 1 < PACK:
                first_product(t + 1)
            if t == 0:
                nc.scalar.activation(h[t][:], h_bank[t][:], COPY, scale=0.0625)
            else:
                nc.vector.tensor_scalar(h[t][:], h_bank[t][:], 0.0625, None, ALU.mult)
            nc.scalar.activation(pair[t][:, :W], h[t][:].indirect(n1_list[:]), COPY)
            nc.scalar.activation(pair[t][:, W:], h[t][:].indirect(n2_list[:]), COPY)

        def polar(t):
            pa, pb = pair[t][:, :W], pair[t][:, W:]
            nc.vector.scalar_tensor_tensor(rb[t][:], pa, -0.5, pb, ALU.mult, ALU.add)
            nc.vector.tensor_tensor(squares[t][:], pair[t][:], pair[t][:], ALU.mult)
            nc.vector.scalar_tensor_tensor(
                radicand[t][:], squares[t][:, :W], 0.25, squares[t][:, W:], ALU.add, ALU.add
            )

        def put_rb(t):
            nc.scalar.activation(dt[t][:].indirect(n2_list[:]), rb[t][:], COPY)
            nc.scalar.activation(ra[t][:], radicand[t][:], SQRT)

        def put_ra(t):
            nc.scalar.activation(dt[t][:].indirect(n1_list[:]), ra[t][:], COPY)
            for cols in halves if t == PACK - 1 else [slice(0, S)]:
                nc.vector.tensor_scalar(z[:, cols, t], dt[t][:, cols], gain[:, t : t + 1], None, ALU.mult)

        first_product(0)
        for step in range(PACK + 2):
            if step < PACK:
                fetch_pairs(step)
                polar(step)
            if 1 <= step <= PACK:
                put_rb(step - 1)
            if step >= 2:
                put_ra(step - 2)

        w1_plane = keep.tile([P, N], U8, name="w1_plane", tag="d_picked", align_bytes=64)
        nc.gpsimd.memset(w1_plane[:].bitcast(I32), 0)
        for q in range(4):
            nc.sync.dma_start(
                w1_plane[32 * q : 32 * q + 4, :].bitcast(I32), w1_scales[0, 4 * q : 4 * q + 4, :].bitcast(I32)
            )

        z_codes = keep.tile([P, S], U32, name="z_codes", align_bytes=64)
        z_plane = keep.tile([P, S], U8, name="z_plane", align_bytes=64)
        for cols in halves:
            nc.vector.quantize_mx(
                out=z_codes[:, cols].bitcast(FP8X4),
                scales=z_plane[:, cols],
                in_=z[:, cols, :].rearrange("p s t -> p (s t)"),
            )

        blocks = N // P
        h2 = [keep.tile([P, S + SPARE], F32, name=f"h2_{u}") for u in range(blocks)]
        other = [keep.tile([P, S], F32, name=f"other{u}") for u in range(blocks)]
        nw = [keep.tile([P, S], F32, name=f"nw{u}") for u in range(blocks)]
        page = [keep.tile([P, U], F32, name=f"page{u}") for u in range(blocks)]
        nc.vector.memset(page[0][:], 0.0)
        for u in range(1, blocks):
            nc.scalar.copy(page[u][:], page[0][:])

        def second_product(u, cols, tag):
            bank = psum.tile([P, cols.stop - cols.start], F32, name="h2_bank", tag=tag)
            nc.tensor.matmul_mx(
                out=bank[:],
                lhsT=w1_codes[:, 2 * u * P : 2 * (u + 1) * P].bitcast(FP4X4),
                lhsT_scale=w1_plane[:, u * P : (u + 1) * P],
                rhs=z_codes[:, cols].bitcast(FP8X4),
                rhs_scale=z_plane[:, cols],
                start=True,
                stop=True,
            )
            return bank

        def fetch_other(u):
            if u == 0:
                for c, cols in enumerate(halves):
                    nc.scalar.activation(h2[u][:, cols], second_product(u, cols, f"half_bank{c}")[:], COPY)
            else:
                nc.vector.tensor_copy(h2[u][:, :S], second_product(u, slice(0, S), f"h_bank{u}")[:])
            nc.scalar.activation(other[u][:], h2[u][:].indirect(n4_list[:]), COPY)
            nc.vector.tensor_tensor(nw[u][:], h2[u][:, :S], other[u][:], ALU.max)

        def put_page(u):
            nc.scalar.activation(page[u][:].indirect(n3_list[:]), nw[u][:], COPY)
            nc.sync.dma_start(out[u * P : (u + 1) * P, :], page[u][:])

        for step in range(blocks + 2):
            if step < blocks:
                fetch_other(step)
            if step >= 2:
                put_page(step - 2)
